import numpy as np
import ml_dtypes


def mxq(x, axis, fmt="e4m3"):
    dtype, down = {"e4m3": (ml_dtypes.float8_e4m3fn, 7), "e5m2": (ml_dtypes.float8_e5m2, 14)}[fmt]
    v = np.moveaxis(np.asarray(x, np.float32).astype(ml_dtypes.bfloat16).astype(np.float64), axis, -1)
    blocks = v.reshape(v.shape[:-1] + (-1, 32))
    amax = np.abs(blocks).max(-1, keepdims=True)
    byte = np.maximum(np.where(amax > 0, np.frexp(amax)[1] - 1 + 127, 0) - down, 1)
    scale = np.exp2(byte - 127.0)
    codes = (blocks / scale).astype(np.float32).astype(dtype).astype(np.float64)
    return np.moveaxis((codes * scale).reshape(v.shape), -1, axis)


WIDE = False


def mx_kscale(k):
    if not WIDE:
        return np.ones(k)
    levels = np.array([10, -10, 5, -5, 0])
    if k % 512:
        return np.exp2(np.random.permutation(np.resize(levels, k // 32))).repeat(32)
    a = np.empty((k // 512, 16))
    for p in range(k // 512):
        a[p, :8] = np.random.permutation(np.resize(levels, 8))
        for g in range(8):
            far = levels[np.abs(levels - a[p, g]) >= 10]
            a[p, g + 8] = far[np.random.randint(len(far))]
    return np.exp2(a.ravel()).repeat(32)


def f64(x):
    return np.asarray(x).astype(np.float64)


def striped(idx):
    return np.tile(idx.reshape(-1, 16).T, (8, 1)).astype(np.uint16)


def unstriped(offs):
    return offs[:16].T.reshape(-1).astype(np.int64)


def pack_weight(w):
    k, n = w.shape
    w = f64(np.asarray(w, np.float32).astype(ml_dtypes.bfloat16)).reshape(k // 32, 32, n)
    amax = np.abs(w).max(1)
    byte = np.clip(np.where(amax > 0, np.frexp(amax)[1] - 1 + 127 - 7, 1), 1, 254)
    scaled = (w * np.exp2(127.0 - byte)[:, None, :]).reshape(k, n).astype(np.float32)
    words = np.ascontiguousarray(scaled.reshape(k // 512, 128, 4, n).transpose(0, 1, 3, 2)).astype(ml_dtypes.float8_e4m3fn).view(np.uint8)
    return words, np.ascontiguousarray(byte.astype(np.uint8).reshape(k // 512, 16, n))


def unpack_weight(words, scales):
    g, p, n, _ = words.shape
    vals = np.ascontiguousarray(words).view(ml_dtypes.float8_e4m3fn).astype(np.float64) * np.repeat(np.exp2(scales.astype(np.float64) - 127.0), 8, axis=1)[..., None]
    return vals.transpose(0, 1, 3, 2).reshape(g * 512, n)


K, T, S, N, U = 1024, 1024, 512, 128, 512
P = 2 ** 7


def setup_inputs():
    n = np.random.standard_normal
    s = mx_kscale(K)[:, None]
    packed_xT = pack_weight(n((K, T)) * s)
    return {
        "x_words": packed_xT[0],
        "x_scales": packed_xT[1],
        "w1": (n((K, N)) / np.sqrt(K) / s).astype(np.float32),
        "w2": (n((K, N)) / np.sqrt(K) / s).astype(np.float32),
        "w3": (n((K, N)) / np.sqrt(K) / s).astype(np.float32),
        "logfk": (np.tile(np.random.uniform(0.1, 0.8, U) * np.where(np.random.uniform(size=U) < 0.5, 1.0, -1.0), (P, 1))).astype(np.float32),
        "mat": (np.tile(np.random.uniform(0.2, 2.0, U), (P, 1))).astype(np.float32),
        "offs": striped(np.random.permutation(T)[:S]),
        "expy": striped(np.random.randint(0, S, U)),
    }


def reference(x_words, x_scales, w1, w2, w3, logfk, mat, offs, expy):
    xq = unpack_weight(x_words, x_scales)[:, unstriped(offs)]
    ya = mxq(f64(w1), 0, "e4m3").T @ xq
    alp = 0.3 * (np.log(np.exp(ya) + 1.0) + 0.3)
    ag = alp[:, unstriped(expy)]
    yv = mxq(f64(w3), 0, "e4m3").T @ xq
    nu = 0.5 * (np.log(np.exp(yv) + 1.0)) + 0.1
    vg = nu[:, unstriped(expy)]
    zr = (vg * f64(logfk)[:1]) / ag
    yr = mxq(f64(w2), 0, "e4m3").T @ xq
    rho = 0.7 * np.tanh(yr)
    rg = rho[:, unstriped(expy)]
    xz = np.log((np.sqrt(-1.0 * (2.0 * (rg * zr)) + 1.0 + (zr) ** 2) + zr - rg) / (-1.0 * rg + 1.0))
    return (((((ag * zr) / xz) * ((0.25 * ((rg * vg) * ag) + (((vg) ** 2) * (-3.0 * ((rg) ** 2) + 2.0)) / 24) * f64(mat)[:1] + 1.0)) ** 2) * f64(mat)[:1]) * (np.exp(0.5 * (-1.0 * ((f64(logfk)[:1]) ** 2))))

@@ -1,0 +1,254 @@
+import math
+from contextlib import ExitStack
+
+import concourse.mybir as mybir
+from concourse.masks import make_identity
+
+K, T, S, N, U = 1024, 1024, 512, 128, 512
+FLOPS = 3 * 2 * K * N * S
+
+F32 = mybir.dt.float32
+BF16 = mybir.dt.bfloat16
+I32 = mybir.dt.int32
+U32 = mybir.dt.uint32
+U16 = mybir.dt.uint16
+U8 = mybir.dt.uint8
+FP8X4 = mybir.dt.float8_e4m3fn_x4
+ALU = mybir.AluOpType
+ACT = mybir.ActivationFunctionType
+
+P = 128
+PACK = 4
+PASSES = K // (P * PACK)
+BLOCKS = U // P
+HALVES = 2
+HALF = U // HALVES
+TINY = 2.0 ** -60
+
+
+def tile_picked_ysabr_var_p_kernel(
+    tc, x_words, x_scales, w1, w2, w3, logfk, mat, offs, expy, out
+):
+    nc = tc.nc
+    vec, act = nc.vector, nc.scalar
+    with ExitStack() as ctx:
+        keep = ctx.enter_context(tc.tile_pool(name="keep", bufs=1))
+        psum = ctx.enter_context(tc.psum_pool(name="psum", bufs=1))
+
+        def wide(name):
+            return keep.tile([P, U], F32, name=name)
+
+        def half(tile, h):
+            return tile[:, h * HALF : (h + 1) * HALF]
+
+        def block(tile, j):
+            return tile[:, j * P : (j + 1) * P]
+
+        def bank(name, b, width=U):
+            return psum.tile([P, width], F32, name=name, tag="bank%d" % b)
+
+        picks = keep.tile([P, S // 16], U16, name="picks")
+        nc.sync.dma_start(picks[:], offs)
+
+        planes = keep.tile([P, T], U8, name="planes", align_bytes=64)
+        nc.gpsimd.memset(planes[:].bitcast(I32), 0)
+        for q in range(4):
+            nc.sync.dma_start(
+                planes[32 * q : 32 * q + 4 * PASSES, :].bitcast(I32),
+                x_scales[:, 4 * q : 4 * q + 4, :].bitcast(I32),
+            )
+        rows = keep.tile([P, P], F32, name="rows")
+        sig_rows = keep.tile([P, P], F32, name="sig_rows")
+        nc.gpsimd.memset(rows[:], 0.0)
+        nc.gpsimd.memset(sig_rows[:], 0.0)
+        k_rows = keep.tile([BLOCKS, P], F32, name="k_rows")
+        nc.sync.dma_start(k_rows[:], logfk[0].rearrange("(j p) -> j p", p=P))
+        sq_rows = keep.tile([BLOCKS, P], F32, name="sq_rows")
+        vec.tensor_tensor(sq_rows[:], k_rows[:], k_rows[:], ALU.mult)
+        vec.tensor_scalar(rows[0:BLOCKS, :], k_rows[:], 5.0 / 3.0, None, ALU.mult)
+        act.activation(sig_rows[0:BLOCKS, :], sq_rows[:], ACT.Sigmoid, scale=-0.5)
+
+        words = [keep.tile([P, T], I32, name="words%d" % o, align_bytes=64) for o in range(PASSES)]
+        raw = {}
+
+        def load_words(o):
+            nc.sync.dma_start(words[o][:], x_words[o].rearrange("p n t -> p (n t)").bitcast(I32))
+
+        def load_weight(name, w, o):
+            raw[name, o] = keep.tile([P, PACK, N], F32, name="raw_%s%d" % (name, o))
+            part = w[o * P * PACK : (o + 1) * P * PACK, :]
+            nc.sync.dma_start(raw[name, o][:], part.rearrange("(p t) c -> p t c", t=PACK))
+
+        def load_whole(name, w):
+            both = keep.tile([P, PASSES, PACK, N], F32, name="raw_" + name)
+            nc.sync.dma_start(both[:], w.rearrange("(o p t) c -> p o t c", p=P, t=PACK))
+            for o in range(PASSES):
+                raw[name, o] = both[:, o]
+
+        load_words(0)
+        load_words(1)
+        load_whole("a", w1)
+        reads = keep.tile([P, U // 16], U16, name="reads")
+        nc.sync.dma_start(reads[:], expy)
+        load_whole("v", w3)
+        load_weight("r", w2, 0)
+        load_weight("r", w2, 1)
+        nc.sync.dma_start(rows[BLOCKS : 2 * BLOCKS, :], mat[0].rearrange("(j p) -> j p", p=P))
+
+        x_codes = [keep.tile([P, S], U32, name="x_codes%d" % o, align_bytes=64) for o in range(PASSES)]
+        x_planes = keep.tile([P, S], U8, name="x_planes", align_bytes=64)
+        for o in range(PASSES):
+            vec.tensor_copy(x_codes[o][:], words[o][:].bitcast(U32).indirect(picks[:]))
+        vec.tensor_copy(x_planes[:], planes[:].indirect(picks[:]))
+
+        ident = keep.tile([P, P], F32, name="ident")
+        make_identity(nc, ident[:])
+
+        def product(name, b, cast_engines):
+            acc = bank("acc_" + name, b)
+            for o in range(PASSES):
+                grouped = keep.tile([P, N, PACK], BF16, name="grouped_%s%d" % (name, o), align_bytes=64)
+                src = raw[name, o][:].rearrange("p t c -> p c t")
+                if cast_engines[o] == "scalar":
+                    act.copy(grouped[:], src)
+                else:
+                    vec.tensor_copy(grouped[:], src)
+                codes = keep.tile([P, N], U32, name="codes_%s%d" % (name, o), align_bytes=64)
+                scales = keep.tile([P, N], U8, name="scales_%s%d" % (name, o), align_bytes=64)
+                vec.quantize_mx(out=codes[:].bitcast(FP8X4), scales=scales[:], in_=grouped[:].rearrange("p c t -> p (c t)"))
+                nc.tensor.matmul_mx(
+                    out=acc[:],
+                    lhsT=codes[:].bitcast(FP8X4),
+                    lhsT_scale=scales[:],
+                    rhs=x_codes[o][:].bitcast(FP8X4),
+                    rhs_scale=x_planes[4 * o : P, :],
+                    start=(o == 0),
+                    stop=(o == PASSES - 1),
+                )
+            return acc
+
+        def fetch(dst, window, h):
+            width = HALF // 16
+            vec.tensor_copy(half(dst, h), window[:].indirect(reads[:, h * width : (h + 1) * width]))
+
+        def turn(dst, h, *terms):
+            for i in range(BLOCKS // HALVES):
+                for n, term in enumerate(terms):
+                    nc.tensor.matmul(
+                        block(dst, i), block(term, h * (BLOCKS // HALVES) + i), ident[:],
+                        start=(n == 0), stop=(n == len(terms) - 1), is_transpose=True,
+                    )
+
+        shift = {"a": 0.3, "v": 0.2}
+        acc_a = product("a", 1, ("scalar", "scalar"))
+        acc_v = product("v", 2, ("scalar", "vector"))
+        window = {"a": wide("window_a"), "v": wide("window_v")}
+        vec.tensor_scalar(window["a"][:], acc_a[:], shift["a"], None, ALU.add)
+        fetched = dict((n, wide("fetched_" + n)) for n in ("a", "v", "r"))
+        gate = {"a": wide("gate_a"), "v": wide("gate_v")}
+        whole_a = bank("turned_a", 0)
+        raw_sum = {"a": [half(whole_a, h) for h in range(HALVES)]}
+        for h in range(HALVES):
+            fetch(fetched["a"], window["a"], h)
+            turn(raw_sum["a"][h], h, fetched["a"])
+        acc_r = product("r", 3, ("scalar", "scalar"))
+        act.activation(window["v"][:], acc_v[:], ACT.Identity, bias=shift["v"])
+        act.activation(gate["a"][:], whole_a[:], ACT.Sigmoid, scale=-1.0, bias=shift["a"])
+        window["r"] = keep.tile([P, S], F32, name="window_r", tag="reused")
+        act.activation(window["r"][:], acc_r[:], ACT.Tanh)
+        raw_sum["v"] = [bank("turned_v%d" % h, (4, 1)[h], HALF)[:] for h in range(HALVES)]
+        for h in range(HALVES):
+            fetch(fetched["v"], window["v"], h)
+            turn(raw_sum["v"][h], h, fetched["v"])
+            act.activation(half(gate["v"], h), raw_sum["v"][h], ACT.Sigmoid, scale=-1.0, bias=shift["v"])
+
+        th = bank("turned_r", 2)
+        r2 = bank("turned_r2", 3)
+        r2_plain = wide("r2_plain")
+        for h in range(HALVES):
+            fetch(fetched["r"], window["r"], h)
+            turn(half(th, h), h, fetched["r"])
+        for h in range(HALVES):
+            vec.scalar_tensor_tensor(half(r2_plain, h), half(fetched["r"], h), 0.49, half(fetched["r"], h), ALU.mult, ALU.mult)
+            turn(half(r2, h), h, r2_plain)
+
+        turned = bank("turned", 5, 2 * P)
+        nc.tensor.transpose(block(turned, 0), rows[:], ident[:])
+        nc.tensor.transpose(block(turned, 1), sig_rows[:], ident[:])
+        cols = keep.tile([P, 2, 2 * BLOCKS], F32, name="cols")
+        vec.tensor_copy(cols[:], turned[:].rearrange("p (a n) -> p a n", a=2)[:, :, : 2 * BLOCKS])
+        k_mul, t_col, sig = cols[:, 0, :BLOCKS], cols[:, 0, BLOCKS:], cols[:, 1, :BLOCKS]
+
+        def small(name):
+            return keep.tile([P, BLOCKS], F32, name=name)
+
+        rest, inv, decay, kt, kkt = [small(n) for n in ("rest", "inv", "decay", "kt", "kkt")]
+        t_mul, c_mul = [small(n) for n in ("t_mul", "c_mul")]
+        vec.tensor_scalar(rest[:], sig, -1.0, 1.0, ALU.mult, ALU.add)
+        vec.tensor_scalar(t_mul[:], t_col, -1.0 / 32.0, None, ALU.mult)
+        vec.reciprocal(inv[:], rest[:])
+        vec.scalar_tensor_tensor(kt[:], k_mul, 0.09, t_col, ALU.mult, ALU.mult)
+        vec.tensor_tensor(decay[:], sig, inv[:], ALU.mult)
+        vec.tensor_tensor(kkt[:], kt[:], k_mul, ALU.mult)
+        vec.tensor_tensor(c_mul[:], decay[:], kkt[:], ALU.mult)
+
+        logs = keep.tile([P, 2 * U], F32, name="logs", tag="reused")
+        log_of = {"a": logs[:, :U], "v": logs[:, U:]}
+        for name in ("a", "v"):
+            for h in range(HALVES):
+                act.activation(half(log_of[name], h), half(gate[name], h), ACT.Ln, scale=math.exp(-shift[name]), bias=TINY)
+
+        names = "a v p w w2 g q a2 ln_d s ln_n y1 y2 y4 y5 hh xz xz2 xz4 t2 res".split()
+        x = dict((name, wide("x_" + name)) for name in names)
+
+        def stt(o, a, c, b, op0, op1):
+            for h in range(HALVES):
+                vec.scalar_tensor_tensor(half(x[o], h), half(a, h), c, half(b, h), op0, op1)
+
+        def tt(o, a, b, op):
+            for h in range(HALVES):
+                vec.tensor_tensor(half(x[o], h), half(a, h), half(b, h), op)
+
+        def by_col(o, a, col, b, op1):
+            for j in range(BLOCKS):
+                vec.scalar_tensor_tensor(block(x[o], j), block(a, j), col[:, j : j + 1], block(b, j), ALU.mult, op1)
+
+        def fn(o, a, func):
+            for h in range(HALVES):
+                act.activation(half(x[o], h), half(a, h), func)
+
+        for h in range(HALVES):
+            vec.scalar_tensor_tensor(half(x["a"], h), half(log_of["a"], h), -1.0, raw_sum["a"][h], ALU.mult, ALU.max)
+        stt("p", th, -0.7, x["a"], ALU.mult, ALU.mult)
+        fn("a2", x["a"], ACT.Square)
+        den = [bank("den%d" % h, 5 + h, HALF) for h in range(HALVES)]
+        for h in range(HALVES):
+            turn(den[h], h, x["a"], x["p"])
+            act.activation(half(x["ln_d"], h), den[h][:], ACT.Ln)
+        for h in range(HALVES):
+            vec.scalar_tensor_tensor(half(x["v"], h), half(log_of["v"], h), -1.0, raw_sum["v"][h], ALU.mult, ALU.max)
+        by_col("w", x["v"], k_mul, x["p"], ALU.add)
+        stt("g", r2, -1.0, x["a2"], ALU.add, ALU.mult)
+        tt("w2", x["w"], x["w"], ALU.mult)
+        tt("q", x["w2"], x["g"], ALU.subtract)
+        fn("s", x["q"], ACT.Sqrt)
+        num = [bank("num%d" % h, (7, 1)[h], HALF) for h in range(HALVES)]
+        for h in range(HALVES):
+            turn(num[h], h, x["w"], x["s"])
+        for h in range(HALVES):
+            act.activation(half(x["ln_n"], h), num[h][:], ACT.Ln)
+        stt("y1", r2, -2.0 / 3.0, x["v"], ALU.add, ALU.mult)
+        stt("y2", x["p"], 1.2, x["y1"], ALU.mult, ALU.add)
+        by_col("y4", x["y2"], t_mul, x["v"], ALU.mult)
+        stt("y5", x["y4"], 1.0, x["v"], ALU.add, ALU.mult)
+        by_col("hh", x["y5"], c_mul, x["y5"], ALU.mult)
+        top = [bank("top%d" % h, (0, 4)[h], HALF) for h in range(HALVES)]
+        for h in range(HALVES):
+            turn(top[h], h, x["hh"])
+        tt("xz", x["ln_n"], x["ln_d"], ALU.subtract)
+        tt("xz2", x["xz"], x["xz"], ALU.mult)
+        tt("xz4", x["xz2"], x["xz2"], ALU.mult)
+        fn("t2", x["xz4"], ACT.Abs_reciprocal_sqrt)
+        for h, queue in enumerate((nc.sync, nc.scalar)):
+            vec.tensor_tensor(half(x["res"], h), half(x["t2"], h), top[h][:], ALU.mult)
+            queue.dma_start(out[:, h * HALF : (h + 1) * HALF], half(x["res"], h))

@@ -52,15 +52,10 @@ def tile_picked_ysabr_var_p_kernel(
 
         planes = keep.tile([P, T], U8, name="planes", align_bytes=64)
         nc.gpsimd.memset(planes[:].bitcast(I32), 0)
-        for q in range(4):
-            nc.sync.dma_start(
-                planes[32 * q : 32 * q + 4 * PASSES, :].bitcast(I32),
-                x_scales[:, 4 * q : 4 * q + 4, :].bitcast(I32),
-            )
         rows = keep.tile([P, P], F32, name="rows")
         sig_rows = keep.tile([P, P], F32, name="sig_rows")
         nc.gpsimd.memset(rows[:], 0.0)
-        nc.gpsimd.memset(sig_rows[:], 0.0)
+        vec.memset(sig_rows[:], 0.0)
         k_rows = keep.tile([BLOCKS, P], F32, name="k_rows")
         nc.sync.dma_start(k_rows[:], logfk[0].rearrange("(j p) -> j p", p=P))
         sq_rows = keep.tile([BLOCKS, P], F32, name="sq_rows")
@@ -86,6 +81,11 @@ def tile_picked_ysabr_var_p_kernel(
                 raw[name, o] = both[:, o]
 
         load_words(0)
+        for q in range(4):
+            nc.sync.dma_start(
+                planes[32 * q : 32 * q + 4 * PASSES, :].bitcast(I32),
+                x_scales[:, 4 * q : 4 * q + 4, :].bitcast(I32),
+            )
         load_words(1)
         load_whole("a", w1)
         reads = keep.tile([P, U // 16], U16, name="reads")
@@ -97,9 +97,9 @@ def tile_picked_ysabr_var_p_kernel(
 
         x_codes = [keep.tile([P, S], U32, name="x_codes%d" % o, align_bytes=64) for o in range(PASSES)]
         x_planes = keep.tile([P, S], U8, name="x_planes", align_bytes=64)
-        for o in range(PASSES):
-            vec.tensor_copy(x_codes[o][:], words[o][:].bitcast(U32).indirect(picks[:]))
+        vec.tensor_copy(x_codes[0][:], words[0][:].bitcast(U32).indirect(picks[:]))
         vec.tensor_copy(x_planes[:], planes[:].indirect(picks[:]))
+        vec.tensor_copy(x_codes[1][:], words[1][:].bitcast(U32).indirect(picks[:]))
 
         ident = keep.tile([P, P], F32, name="ident")
         make_identity(nc, ident[:])
@@ -108,11 +108,12 @@ def tile_picked_ysabr_var_p_kernel(
             acc = bank("acc_" + name, b)
             for o in range(PASSES):
                 grouped = keep.tile([P, N, PACK], BF16, name="grouped_%s%d" % (name, o), align_bytes=64)
-                src = raw[name, o][:].rearrange("p t c -> p c t")
+                src = raw[name, o][:].rearrange("p t (c i) -> p c t i", i=PACK)
+                dst = grouped[:].rearrange("p (c i) t -> p c t i", i=PACK)
                 if cast_engines[o] == "scalar":
-                    act.copy(grouped[:], src)
+                    act.copy(dst, src)
                 else:
-                    vec.tensor_copy(grouped[:], src)
+                    vec.tensor_copy(dst, src)
                 codes = keep.tile([P, N], U32, name="codes_%s%d" % (name, o), align_bytes=64)
                 scales = keep.tile([P, N], U8, name="scales_%s%d" % (name, o), align_bytes=64)
                 vec.quantize_mx(out=codes[:].bitcast(FP8X4), scales=scales[:], in_=grouped[:].rearrange("p c t -> p (c t)"))
@@ -141,41 +142,39 @@ def tile_picked_ysabr_var_p_kernel(
 
         shift = {"a": 0.3, "v": 0.2}
         acc_a = product("a", 1, ("scalar", "scalar"))
-        acc_v = product("v", 2, ("scalar", "vector"))
+        acc_v = product("v", 2, ("scalar", "scalar"))
         window = {"a": wide("window_a"), "v": wide("window_v")}
-        vec.tensor_scalar(window["a"][:], acc_a[:], shift["a"], None, ALU.add)
-        fetched = dict((n, wide("fetched_" + n)) for n in ("a", "v", "r"))
+        act.activation(window["a"][:], acc_a[:], ACT.Identity, bias=shift["a"])
+        acc_r = product("r", 3, ("vector", "vector"))
+        act.activation(window["v"][:], acc_v[:], ACT.Identity, bias=shift["v"])
+        window["r"] = wide("window_r")
+        act.activation(window["r"][:], acc_r[:], ACT.Tanh)
+        fetched = {"v": wide("fetched_v")}
+        fetched["a"] = keep.tile([P, U], F32, name="fetched_a", tag="grouped_r1", align_bytes=64)
         gate = {"a": wide("gate_a"), "v": wide("gate_v")}
-        whole_a = bank("turned_a", 0)
+        whole_a = bank("turned_a", 5)
         raw_sum = {"a": [half(whole_a, h) for h in range(HALVES)]}
         for h in range(HALVES):
             fetch(fetched["a"], window["a"], h)
             turn(raw_sum["a"][h], h, fetched["a"])
-        acc_r = product("r", 3, ("scalar", "scalar"))
-        act.activation(window["v"][:], acc_v[:], ACT.Identity, bias=shift["v"])
         act.activation(gate["a"][:], whole_a[:], ACT.Sigmoid, scale=-1.0, bias=shift["a"])
-        window["r"] = keep.tile([P, S], F32, name="window_r", tag="reused")
-        act.activation(window["r"][:], acc_r[:], ACT.Tanh)
         raw_sum["v"] = [bank("turned_v%d" % h, (4, 1)[h], HALF)[:] for h in range(HALVES)]
         for h in range(HALVES):
             fetch(fetched["v"], window["v"], h)
             turn(raw_sum["v"][h], h, fetched["v"])
             act.activation(half(gate["v"], h), raw_sum["v"][h], ACT.Sigmoid, scale=-1.0, bias=shift["v"])
 
-        th = bank("turned_r", 2)
-        r2 = bank("turned_r2", 3)
-        r2_plain = wide("r2_plain")
+        th = bank("turned_r", 0)
+        r2 = wide("r2")
+        fetched["r"] = keep.tile([P, U], F32, name="fetched_r", tag="window_v")
         for h in range(HALVES):
             fetch(fetched["r"], window["r"], h)
             turn(half(th, h), h, fetched["r"])
-        for h in range(HALVES):
-            vec.scalar_tensor_tensor(half(r2_plain, h), half(fetched["r"], h), 0.49, half(fetched["r"], h), ALU.mult, ALU.mult)
-            turn(half(r2, h), h, r2_plain)
 
-        turned = bank("turned", 5, 2 * P)
+        turned = bank("turned", 2, 2 * P)
         nc.tensor.transpose(block(turned, 0), rows[:], ident[:])
         nc.tensor.transpose(block(turned, 1), sig_rows[:], ident[:])
-        cols = keep.tile([P, 2, 2 * BLOCKS], F32, name="cols")
+        cols = keep.tile([P, 2, 2 * BLOCKS], F32, name="cols", tag="window_r")
         vec.tensor_copy(cols[:], turned[:].rearrange("p (a n) -> p a n", a=2)[:, :, : 2 * BLOCKS])
         k_mul, t_col, sig = cols[:, 0, :BLOCKS], cols[:, 0, BLOCKS:], cols[:, 1, :BLOCKS]
 
@@ -192,7 +191,7 @@ def tile_picked_ysabr_var_p_kernel(
         vec.tensor_tensor(kkt[:], kt[:], k_mul, ALU.mult)
         vec.tensor_tensor(c_mul[:], decay[:], kkt[:], ALU.mult)
 
-        logs = keep.tile([P, 2 * U], F32, name="logs", tag="reused")
+        logs = keep.tile([P, 2 * U], F32, name="logs", tag="fetched_v")
         log_of = {"a": logs[:, :U], "v": logs[:, U:]}
         for name in ("a", "v"):
             for h in range(HALVES):
@@ -220,7 +219,8 @@ def tile_picked_ysabr_var_p_kernel(
         for h in range(HALVES):
             vec.scalar_tensor_tensor(half(x["a"], h), half(log_of["a"], h), -1.0, raw_sum["a"][h], ALU.mult, ALU.max)
         stt("p", th, -0.7, x["a"], ALU.mult, ALU.mult)
-        fn("a2", x["a"], ACT.Square)
+        act.activation(x["a2"][:], x["a"][:], ACT.Square)
+        act.activation(r2[:], th[:], ACT.Square, scale=0.7)
         den = [bank("den%d" % h, 5 + h, HALF) for h in range(HALVES)]
         for h in range(HALVES):
             turn(den[h], h, x["a"], x["p"])

@@ -53,15 +53,18 @@ def tile_picked_ysabr_var_p_kernel(
         planes = keep.tile([P, T], U8, name="planes", align_bytes=64)
         nc.gpsimd.memset(planes[:].bitcast(I32), 0)
         rows = keep.tile([P, P], F32, name="rows")
-        sig_rows = keep.tile([P, P], F32, name="sig_rows")
+        made_rows = keep.tile([P, 2, P], F32, name="made_rows")
         nc.gpsimd.memset(rows[:], 0.0)
-        vec.memset(sig_rows[:], 0.0)
+        vec.memset(made_rows[:], 0.0)
         k_rows = keep.tile([BLOCKS, P], F32, name="k_rows")
         nc.sync.dma_start(k_rows[:], logfk[0].rearrange("(j p) -> j p", p=P))
         sq_rows = keep.tile([BLOCKS, P], F32, name="sq_rows")
         vec.tensor_tensor(sq_rows[:], k_rows[:], k_rows[:], ALU.mult)
         vec.tensor_scalar(rows[0:BLOCKS, :], k_rows[:], 5.0 / 3.0, None, ALU.mult)
-        act.activation(sig_rows[0:BLOCKS, :], sq_rows[:], ACT.Sigmoid, scale=-0.5)
+        sig_rows = keep.tile([BLOCKS, P], F32, name="sig_rows")
+        act.activation(sig_rows[:], sq_rows[:], ACT.Sigmoid, scale=-0.5)
+        act.activation(made_rows[0:BLOCKS, 0, :], sig_rows[:], ACT.Identity, scale=-1.0, bias=1.0)
+        vec.scalar_tensor_tensor(made_rows[0:BLOCKS, 1, :], sig_rows[:], 0.25 / 1024.0, sq_rows[:], ALU.mult, ALU.mult)
 
         words = [keep.tile([P, T], I32, name="words%d" % o, align_bytes=64) for o in range(PASSES)]
         raw = {}
@@ -87,7 +90,8 @@ def tile_picked_ysabr_var_p_kernel(
                 x_scales[:, 4 * q : 4 * q + 4, :].bitcast(I32),
             )
         load_words(1)
-        load_whole("a", w1)
+        load_weight("a", w1, 0)
+        load_weight("a", w1, 1)
         reads = keep.tile([P, U // 16], U16, name="reads")
         nc.sync.dma_start(reads[:], expy)
         load_whole("v", w3)
@@ -143,7 +147,7 @@ def tile_picked_ysabr_var_p_kernel(
         shift = {"a": 0.3, "v": 0.2}
         acc_a = product("a", 1, ("scalar", "scalar"))
         acc_v = product("v", 2, ("scalar", "scalar"))
-        window = {"a": wide("window_a"), "v": wide("window_v")}
+        window = {"a": keep.tile([P, S], F32, name="window_a", tag="raw_v"), "v": wide("window_v")}
         act.activation(window["a"][:], acc_a[:], ACT.Identity, bias=shift["a"])
         acc_r = product("r", 3, ("vector", "vector"))
         act.activation(window["v"][:], acc_v[:], ACT.Identity, bias=shift["v"])
@@ -152,17 +156,18 @@ def tile_picked_ysabr_var_p_kernel(
         fetched = {"v": wide("fetched_v")}
         fetched["a"] = keep.tile([P, U], F32, name="fetched_a", tag="grouped_r1", align_bytes=64)
         gate = {"a": wide("gate_a"), "v": wide("gate_v")}
-        whole_a = bank("turned_a", 5)
-        raw_sum = {"a": [half(whole_a, h) for h in range(HALVES)]}
-        for h in range(HALVES):
-            fetch(fetched["a"], window["a"], h)
-            turn(raw_sum["a"][h], h, fetched["a"])
-        act.activation(gate["a"][:], whole_a[:], ACT.Sigmoid, scale=-1.0, bias=shift["a"])
-        raw_sum["v"] = [bank("turned_v%d" % h, (4, 1)[h], HALF)[:] for h in range(HALVES)]
-        for h in range(HALVES):
-            fetch(fetched["v"], window["v"], h)
-            turn(raw_sum["v"][h], h, fetched["v"])
-            act.activation(half(gate["v"], h), raw_sum["v"][h], ACT.Sigmoid, scale=-1.0, bias=shift["v"])
+        for name in ("a", "v"):
+            for h in range(HALVES):
+                fetch(fetched[name], window[name], h)
+                act.activation(half(gate[name], h), half(fetched[name], h), ACT.Sigmoid, scale=-1.0, bias=shift[name])
+        raw_t = {"a": bank("raw_a_t", 5), "v": bank("raw_v_t", 1)}
+        gate_t = {"a": bank("gate_a_t", 4), "v": bank("gate_v_t", 7)}
+        for name in ("a", "v"):
+            for h in range(HALVES):
+                turn(half(gate_t[name], h), h, gate[name])
+            for h in range(HALVES):
+                turn(half(raw_t[name], h), h, fetched[name])
+        raw_sum = dict((name, [half(raw_t[name], h) for h in range(HALVES)]) for name in ("a", "v"))
 
         th = bank("turned_r", 0)
         r2 = wide("r2")
@@ -171,31 +176,23 @@ def tile_picked_ysabr_var_p_kernel(
             fetch(fetched["r"], window["r"], h)
             turn(half(th, h), h, fetched["r"])
 
-        turned = bank("turned", 2, 2 * P)
+        turned = bank("turned", 2, 3 * P)
         nc.tensor.transpose(block(turned, 0), rows[:], ident[:])
-        nc.tensor.transpose(block(turned, 1), sig_rows[:], ident[:])
-        cols = keep.tile([P, 2, 2 * BLOCKS], F32, name="cols", tag="window_r")
-        vec.tensor_copy(cols[:], turned[:].rearrange("p (a n) -> p a n", a=2)[:, :, : 2 * BLOCKS])
-        k_mul, t_col, sig = cols[:, 0, :BLOCKS], cols[:, 0, BLOCKS:], cols[:, 1, :BLOCKS]
-
-        def small(name):
-            return keep.tile([P, BLOCKS], F32, name=name)
-
-        rest, inv, decay, kt, kkt = [small(n) for n in ("rest", "inv", "decay", "kt", "kkt")]
-        t_mul, c_mul = [small(n) for n in ("t_mul", "c_mul")]
-        vec.tensor_scalar(rest[:], sig, -1.0, 1.0, ALU.mult, ALU.add)
-        vec.tensor_scalar(t_mul[:], t_col, -1.0 / 32.0, None, ALU.mult)
-        vec.reciprocal(inv[:], rest[:])
-        vec.scalar_tensor_tensor(kt[:], k_mul, 0.09, t_col, ALU.mult, ALU.mult)
-        vec.tensor_tensor(decay[:], sig, inv[:], ALU.mult)
-        vec.tensor_tensor(kkt[:], kt[:], k_mul, ALU.mult)
-        vec.tensor_tensor(c_mul[:], decay[:], kkt[:], ALU.mult)
+        for i in range(2):
+            nc.tensor.transpose(block(turned, 1 + i), made_rows[:, i, :], ident[:])
+        cols = keep.tile([P, 3, 2 * BLOCKS], F32, name="cols", tag="window_r")
+        vec.tensor_copy(cols[:], turned[:].rearrange("p (a n) -> p a n", a=3)[:, :, : 2 * BLOCKS])
+        k_mul, t_mul = cols[:, 0, :BLOCKS], cols[:, 0, BLOCKS:]
+        inv, part, c_mul = [keep.tile([P, BLOCKS], F32, name=n) for n in ("inv", "part", "c_mul")]
+        vec.reciprocal(inv[:], cols[:, 1, :BLOCKS])
+        vec.tensor_tensor(part[:], cols[:, 2, :BLOCKS], t_mul, ALU.mult)
+        vec.tensor_tensor(c_mul[:], part[:], inv[:], ALU.mult)
 
         logs = keep.tile([P, 2 * U], F32, name="logs", tag="fetched_v")
         log_of = {"a": logs[:, :U], "v": logs[:, U:]}
         for name in ("a", "v"):
             for h in range(HALVES):
-                act.activation(half(log_of[name], h), half(gate[name], h), ACT.Ln, scale=math.exp(-shift[name]), bias=TINY)
+                act.activation(half(log_of[name], h), half(gate_t[name], h), ACT.Ln, scale=math.exp(-shift[name]), bias=TINY)
 
         names = "a v p w w2 g q a2 ln_d s ln_n y1 y2 y4 y5 hh xz xz2 xz4 t2 res".split()
         x = dict((name, wide("x_" + name)) for name in names)
@@ -221,7 +218,7 @@ def tile_picked_ysabr_var_p_kernel(
         stt("p", th, -0.7, x["a"], ALU.mult, ALU.mult)
         act.activation(x["a2"][:], x["a"][:], ACT.Square)
         act.activation(r2[:], th[:], ACT.Square, scale=0.7)
-        den = [bank("den%d" % h, 5 + h, HALF) for h in range(HALVES)]
+        den = [bank("den%d" % h, (3, 6)[h], HALF) for h in range(HALVES)]
         for h in range(HALVES):
             turn(den[h], h, x["a"], x["p"])
             act.activation(half(x["ln_d"], h), den[h][:], ACT.Ln)
@@ -232,7 +229,7 @@ def tile_picked_ysabr_var_p_kernel(
         tt("w2", x["w"], x["w"], ALU.mult)
         tt("q", x["w2"], x["g"], ALU.subtract)
         fn("s", x["q"], ACT.Sqrt)
-        num = [bank("num%d" % h, (7, 1)[h], HALF) for h in range(HALVES)]
+        num = [bank("num%d" % h, (7, 5)[h], HALF) for h in range(HALVES)]
         for h in range(HALVES):
             turn(num[h], h, x["w"], x["s"])
         for h in range(HALVES):
@@ -240,7 +237,7 @@ def tile_picked_ysabr_var_p_kernel(
         stt("y1", r2, -2.0 / 3.0, x["v"], ALU.add, ALU.mult)
         stt("y2", x["p"], 1.2, x["y1"], ALU.mult, ALU.add)
         by_col("y4", x["y2"], t_mul, x["v"], ALU.mult)
-        stt("y5", x["y4"], 1.0, x["v"], ALU.add, ALU.mult)
+        stt("y5", x["y4"], -32.0, x["v"], ALU.add, ALU.mult)
         by_col("hh", x["y5"], c_mul, x["y5"], ALU.mult)
         top = [bank("top%d" % h, (0, 4)[h], HALF) for h in range(HALVES)]
         for h in range(HALVES):
@@ -248,7 +245,8 @@ def tile_picked_ysabr_var_p_kernel(
         tt("xz", x["ln_n"], x["ln_d"], ALU.subtract)
         tt("xz2", x["xz"], x["xz"], ALU.mult)
         tt("xz4", x["xz2"], x["xz2"], ALU.mult)
-        fn("t2", x["xz4"], ACT.Abs_reciprocal_sqrt)
-        for h, queue in enumerate((nc.sync, nc.scalar)):
-            vec.tensor_tensor(half(x["res"], h), half(x["t2"], h), top[h][:], ALU.mult)
-            queue.dma_start(out[:, h * HALF : (h + 1) * HALF], half(x["res"], h))
+        for lo, hi in ((0, HALF), (HALF, HALF + P), (HALF + P, U)):
+            h = lo // HALF
+            act.activation(x["t2"][:, lo:hi], x["xz4"][:, lo:hi], ACT.Abs_reciprocal_sqrt)
+            vec.tensor_tensor(x["res"][:, lo:hi], x["t2"][:, lo:hi], top[h][:, lo - h * HALF : hi - h * HALF], ALU.mult)
+            nc.sync.dma_start(out[:, lo:hi], x["res"][:, lo:hi])

@@ -170,11 +170,15 @@ def tile_picked_ysabr_var_p_kernel(
         raw_sum = dict((name, [half(raw_t[name], h) for h in range(HALVES)]) for name in ("a", "v"))
 
         th = bank("turned_r", 0)
-        r2 = wide("r2")
+        r2 = bank("turned_r2", 6)
+        r2_plain = wide("r2_plain")
         fetched["r"] = keep.tile([P, U], F32, name="fetched_r", tag="window_v")
         for h in range(HALVES):
             fetch(fetched["r"], window["r"], h)
             turn(half(th, h), h, fetched["r"])
+        for h in range(HALVES):
+            vec.scalar_tensor_tensor(half(r2_plain, h), half(fetched["r"], h), 0.49, half(fetched["r"], h), ALU.mult, ALU.mult)
+            turn(half(r2, h), h, r2_plain)
 
         turned = bank("turned", 2, 3 * P)
         nc.tensor.transpose(block(turned, 0), rows[:], ident[:])
@@ -217,11 +221,11 @@ def tile_picked_ysabr_var_p_kernel(
             vec.scalar_tensor_tensor(half(x["a"], h), half(log_of["a"], h), -1.0, raw_sum["a"][h], ALU.mult, ALU.max)
         stt("p", th, -0.7, x["a"], ALU.mult, ALU.mult)
         act.activation(x["a2"][:], x["a"][:], ACT.Square)
-        act.activation(r2[:], th[:], ACT.Square, scale=0.7)
-        den = [bank("den%d" % h, (3, 6)[h], HALF) for h in range(HALVES)]
+        act.activation(x["ln_d"][:], x["a"][:], ACT.Ln)
+        act.activation(log_of["a"], th[:], ACT.Ln, scale=-0.7, bias=1.0)
+        den = bank("den", 3)
         for h in range(HALVES):
-            turn(den[h], h, x["a"], x["p"])
-            act.activation(half(x["ln_d"], h), den[h][:], ACT.Ln)
+            turn(half(den, h), h, x["ln_d"], log_of["a"])
         for h in range(HALVES):
             vec.scalar_tensor_tensor(half(x["v"], h), half(log_of["v"], h), -1.0, raw_sum["v"][h], ALU.mult, ALU.max)
         by_col("w", x["v"], k_mul, x["p"], ALU.add)
@@ -242,7 +246,7 @@ def tile_picked_ysabr_var_p_kernel(
         top = [bank("top%d" % h, (0, 4)[h], HALF) for h in range(HALVES)]
         for h in range(HALVES):
             turn(top[h], h, x["hh"])
-        tt("xz", x["ln_n"], x["ln_d"], ALU.subtract)
+        tt("xz", x["ln_n"], den, ALU.subtract)
         tt("xz2", x["xz"], x["xz"], ALU.mult)
         tt("xz4", x["xz2"], x["xz2"], ALU.mult)
         for lo, hi in ((0, HALF), (HALF, HALF + P), (HALF + P, U)):

import math
from contextlib import ExitStack

import concourse.mybir as mybir
from concourse.masks import make_identity

K, T, S, N, U = 1024, 1024, 512, 128, 512
FLOPS = 3 * 2 * K * N * S

F32 = mybir.dt.float32
BF16 = mybir.dt.bfloat16
I32 = mybir.dt.int32
U32 = mybir.dt.uint32
U16 = mybir.dt.uint16
U8 = mybir.dt.uint8
FP8X4 = mybir.dt.float8_e4m3fn_x4
ALU = mybir.AluOpType
ACT = mybir.ActivationFunctionType

P = 128
PACK = 4
PASSES = K // (P * PACK)
BLOCKS = U // P
HALVES = 2
HALF = U // HALVES
TINY = 2.0 ** -60


def tile_picked_ysabr_var_p_kernel(
    tc, x_words, x_scales, w1, w2, w3, logfk, mat, offs, expy, out
):
    nc = tc.nc
    vec, act = nc.vector, nc.scalar
    with ExitStack() as ctx:
        keep = ctx.enter_context(tc.tile_pool(name="keep", bufs=1))
        psum = ctx.enter_context(tc.psum_pool(name="psum", bufs=1))

        def wide(name):
            return keep.tile([P, U], F32, name=name)

        def half(tile, h):
            return tile[:, h * HALF : (h + 1) * HALF]

        def block(tile, j):
            return tile[:, j * P : (j + 1) * P]

        def bank(name, b, width=U):
            return psum.tile([P, width], F32, name=name, tag="bank%d" % b)

        picks = keep.tile([P, S // 16], U16, name="picks")
        nc.sync.dma_start(picks[:], offs)

        planes = keep.tile([P, T], U8, name="planes", align_bytes=64)
        nc.gpsimd.memset(planes[:].bitcast(I32), 0)
        rows = keep.tile([P, P], F32, name="rows")
        made_rows = keep.tile([P, 2, P], F32, name="made_rows")
        nc.gpsimd.memset(rows[:], 0.0)
        vec.memset(made_rows[:], 0.0)
        k_rows = keep.tile([BLOCKS, P], F32, name="k_rows")
        nc.sync.dma_start(k_rows[:], logfk[0].rearrange("(j p) -> j p", p=P))
        sq_rows = keep.tile([BLOCKS, P], F32, name="sq_rows")
        vec.tensor_tensor(sq_rows[:], k_rows[:], k_rows[:], ALU.mult)
        vec.tensor_scalar(rows[0:BLOCKS, :], k_rows[:], 5.0 / 3.0, None, ALU.mult)
        sig_rows = keep.tile([BLOCKS, P], F32, name="sig_rows")
        act.activation(sig_rows[:], sq_rows[:], ACT.Sigmoid, scale=-0.5)
        act.activation(made_rows[0:BLOCKS, 0, :], sig_rows[:], ACT.Identity, scale=-1.0, bias=1.0)
        vec.scalar_tensor_tensor(made_rows[0:BLOCKS, 1, :], sig_rows[:], 0.25 / 1024.0, sq_rows[:], ALU.mult, ALU.mult)

        words = [keep.tile([P, T], I32, name="words%d" % o, align_bytes=64) for o in range(PASSES)]
        raw = {}

        def load_words(o):
            nc.sync.dma_start(words[o][:], x_words[o].rearrange("p n t -> p (n t)").bitcast(I32))

        def load_weight(name, w, o):
            raw[name, o] = keep.tile([P, PACK, N], F32, name="raw_%s%d" % (name, o))
            part = w[o * P * PACK : (o + 1) * P * PACK, :]
            nc.sync.dma_start(raw[name, o][:], part.rearrange("(p t) c -> p t c", t=PACK))

        def load_whole(name, w):
            both = keep.tile([P, PASSES, PACK, N], F32, name="raw_" + name)
            nc.sync.dma_start(both[:], w.rearrange("(o p t) c -> p o t c", p=P, t=PACK))
            for o in range(PASSES):
                raw[name, o] = both[:, o]

        load_words(0)
        for q in range(4):
            nc.sync.dma_start(
                planes[32 * q : 32 * q + 4 * PASSES, :].bitcast(I32),
                x_scales[:, 4 * q : 4 * q + 4, :].bitcast(I32),
            )
        load_words(1)
        load_weight("a", w1, 0)
        load_weight("a", w1, 1)
        reads = keep.tile([P, U // 16], U16, name="reads")
        nc.sync.dma_start(reads[:], expy)
        load_whole("v", w3)
        load_weight("r", w2, 0)
        load_weight("r", w2, 1)
        nc.sync.dma_start(rows[BLOCKS : 2 * BLOCKS, :], mat[0].rearrange("(j p) -> j p", p=P))

        x_codes = [keep.tile([P, S], U32, name="x_codes%d" % o, align_bytes=64) for o in range(PASSES)]
        x_planes = keep.tile([P, S], U8, name="x_planes", align_bytes=64)
        vec.tensor_copy(x_codes[0][:], words[0][:].bitcast(U32).indirect(picks[:]))
        vec.tensor_copy(x_planes[:], planes[:].indirect(picks[:]))
        vec.tensor_copy(x_codes[1][:], words[1][:].bitcast(U32).indirect(picks[:]))

        ident = keep.tile([P, P], F32, name="ident")
        make_identity(nc, ident[:])

        def product(name, b, cast_engines):
            acc = bank("acc_" + name, b)
            for o in range(PASSES):
                grouped = keep.tile([P, N, PACK], BF16, name="grouped_%s%d" % (name, o), align_bytes=64)
                src = raw[name, o][:].rearrange("p t (c i) -> p c t i", i=PACK)
                dst = grouped[:].rearrange("p (c i) t -> p c t i", i=PACK)
                if cast_engines[o] == "scalar":
                    act.copy(dst, src)
                else:
                    vec.tensor_copy(dst, src)
                codes = keep.tile([P, N], U32, name="codes_%s%d" % (name, o), align_bytes=64)
                scales = keep.tile([P, N], U8, name="scales_%s%d" % (name, o), align_bytes=64)
                vec.quantize_mx(out=codes[:].bitcast(FP8X4), scales=scales[:], in_=grouped[:].rearrange("p c t -> p (c t)"))
                nc.tensor.matmul_mx(
                    out=acc[:],
                    lhsT=codes[:].bitcast(FP8X4),
                    lhsT_scale=scales[:],
                    rhs=x_codes[o][:].bitcast(FP8X4),
                    rhs_scale=x_planes[4 * o : P, :],
                    start=(o == 0),
                    stop=(o == PASSES - 1),
                )
            return acc

        def fetch(dst, window, h):
            width = HALF // 16
            vec.tensor_copy(half(dst, h), window[:].indirect(reads[:, h * width : (h + 1) * width]))

        def turn(dst, h, *terms):
            for i in range(BLOCKS // HALVES):
                for n, term in enumerate(terms):
                    nc.tensor.matmul(
                        block(dst, i), block(term, h * (BLOCKS // HALVES) + i), ident[:],
                        start=(n == 0), stop=(n == len(terms) - 1), is_transpose=True,
                    )

        shift = {"a": 0.3, "v": 0.2}
        acc_a = product("a", 1, ("scalar", "scalar"))
        acc_v = product("v", 2, ("scalar", "scalar"))
        window = {"a": keep.tile([P, S], F32, name="window_a", tag="raw_v"), "v": wide("window_v")}
        act.activation(window["a"][:], acc_a[:], ACT.Identity, bias=shift["a"])
        acc_r = product("r", 3, ("vector", "vector"))
        act.activation(window["v"][:], acc_v[:], ACT.Identity, bias=shift["v"])
        window["r"] = wide("window_r")
        act.activation(window["r"][:], acc_r[:], ACT.Tanh)
        fetched = {"v": wide("fetched_v")}
        fetched["a"] = keep.tile([P, U], F32, name="fetched_a", tag="grouped_r1", align_bytes=64)
        gate = {"a": wide("gate_a"), "v": wide("gate_v")}
        for name in ("a", "v"):
            for h in range(HALVES):
                fetch(fetched[name], window[name], h)
                act.activation(half(gate[name], h), half(fetched[name], h), ACT.Sigmoid, scale=-1.0, bias=shift[name])
        raw_t = {"a": bank("raw_a_t", 5), "v": bank("raw_v_t", 1)}
        gate_t = {"a": bank("gate_a_t", 4), "v": bank("gate_v_t", 7)}
        for name in ("a", "v"):
            for h in range(HALVES):
                turn(half(gate_t[name], h), h, gate[name])
            for h in range(HALVES):
                turn(half(raw_t[name], h), h, fetched[name])
        raw_sum = dict((name, [half(raw_t[name], h) for h in range(HALVES)]) for name in ("a", "v"))

        th = bank("turned_r", 0)
        r2 = bank("turned_r2", 6)
        r2_plain = wide("r2_plain")
        fetched["r"] = keep.tile([P, U], F32, name="fetched_r", tag="window_v")
        for h in range(HALVES):
            fetch(fetched["r"], window["r"], h)
            turn(half(th, h), h, fetched["r"])
        for h in range(HALVES):
            vec.scalar_tensor_tensor(half(r2_plain, h), half(fetched["r"], h), 0.49, half(fetched["r"], h), ALU.mult, ALU.mult)
            turn(half(r2, h), h, r2_plain)

        turned = bank("turned", 2, 3 * P)
        nc.tensor.transpose(block(turned, 0), rows[:], ident[:])
        for i in range(2):
            nc.tensor.transpose(block(turned, 1 + i), made_rows[:, i, :], ident[:])
        cols = keep.tile([P, 3, 2 * BLOCKS], F32, name="cols", tag="window_r")
        vec.tensor_copy(cols[:], turned[:].rearrange("p (a n) -> p a n", a=3)[:, :, : 2 * BLOCKS])
        k_mul, t_mul = cols[:, 0, :BLOCKS], cols[:, 0, BLOCKS:]
        inv, part, c_mul = [keep.tile([P, BLOCKS], F32, name=n) for n in ("inv", "part", "c_mul")]
        vec.reciprocal(inv[:], cols[:, 1, :BLOCKS])
        vec.tensor_tensor(part[:], cols[:, 2, :BLOCKS], t_mul, ALU.mult)
        vec.tensor_tensor(c_mul[:], part[:], inv[:], ALU.mult)

        logs = keep.tile([P, 2 * U], F32, name="logs", tag="fetched_v")
        log_of = {"a": logs[:, :U], "v": logs[:, U:]}
        for name in ("a", "v"):
            for h in range(HALVES):
                act.activation(half(log_of[name], h), half(gate_t[name], h), ACT.Ln, scale=math.exp(-shift[name]), bias=TINY)

        names = "a v p w w2 g q a2 ln_d s ln_n y1 y2 y4 y5 hh xz xz2 xz4 t2 res".split()
        x = dict((name, wide("x_" + name)) for name in names)

        def stt(o, a, c, b, op0, op1):
            for h in range(HALVES):
                vec.scalar_tensor_tensor(half(x[o], h), half(a, h), c, half(b, h), op0, op1)

        def tt(o, a, b, op):
            for h in range(HALVES):
                vec.tensor_tensor(half(x[o], h), half(a, h), half(b, h), op)

        def by_col(o, a, col, b, op1):
            for j in range(BLOCKS):
                vec.scalar_tensor_tensor(block(x[o], j), block(a, j), col[:, j : j + 1], block(b, j), ALU.mult, op1)

        def fn(o, a, func):
            for h in range(HALVES):
                act.activation(half(x[o], h), half(a, h), func)

        for h in range(HALVES):
            vec.scalar_tensor_tensor(half(x["a"], h), half(log_of["a"], h), -1.0, raw_sum["a"][h], ALU.mult, ALU.max)
        stt("p", th, -0.7, x["a"], ALU.mult, ALU.mult)
        act.activation(x["a2"][:], x["a"][:], ACT.Square)
        act.activation(x["ln_d"][:], x["a"][:], ACT.Ln)
        act.activation(log_of["a"], th[:], ACT.Ln, scale=-0.7, bias=1.0)
        den = bank("den", 3)
        for h in range(HALVES):
            turn(half(den, h), h, x["ln_d"], log_of["a"])
        for h in range(HALVES):
            vec.scalar_tensor_tensor(half(x["v"], h), half(log_of["v"], h), -1.0, raw_sum["v"][h], ALU.mult, ALU.max)
        by_col("w", x["v"], k_mul, x["p"], ALU.add)
        stt("g", r2, -1.0, x["a2"], ALU.add, ALU.mult)
        tt("w2", x["w"], x["w"], ALU.mult)
        tt("q", x["w2"], x["g"], ALU.subtract)
        fn("s", x["q"], ACT.Sqrt)
        num = [bank("num%d" % h, (7, 5)[h], HALF) for h in range(HALVES)]
        for h in range(HALVES):
            turn(num[h], h, x["w"], x["s"])
        for h in range(HALVES):
            act.activation(half(x["ln_n"], h), num[h][:], ACT.Ln)
        stt("y1", r2, -2.0 / 3.0, x["v"], ALU.add, ALU.mult)
        stt("y2", x["p"], 1.2, x["y1"], ALU.mult, ALU.add)
        by_col("y4", x["y2"], t_mul, x["v"], ALU.mult)
        stt("y5", x["y4"], -32.0, x["v"], ALU.add, ALU.mult)
        by_col("hh", x["y5"], c_mul, x["y5"], ALU.mult)
        top = [bank("top%d" % h, (0, 4)[h], HALF) for h in range(HALVES)]
        for h in range(HALVES):
            turn(top[h], h, x["hh"])
        tt("xz", x["ln_n"], den, ALU.subtract)
        tt("xz2", x["xz"], x["xz"], ALU.mult)
        tt("xz4", x["xz2"], x["xz2"], ALU.mult)
        for lo, hi in ((0, HALF), (HALF, HALF + P), (HALF + P, U)):
            h = lo // HALF
            act.activation(x["t2"][:, lo:hi], x["xz4"][:, lo:hi], ACT.Abs_reciprocal_sqrt)
            vec.tensor_tensor(x["res"][:, lo:hi], x["t2"][:, lo:hi], top[h][:, lo - h * HALF : hi - h * HALF], ALU.mult)
            nc.sync.dma_start(out[:, lo:hi], x["res"][:, lo:hi])
